import numpy as np
import ml_dtypes


def mxq(x, axis, fmt="e4m3"):
    dtype, down = {"e4m3": (ml_dtypes.float8_e4m3fn, 7), "e5m2": (ml_dtypes.float8_e5m2, 14)}[fmt]
    v = np.moveaxis(np.asarray(x, np.float32).astype(ml_dtypes.bfloat16).astype(np.float64), axis, -1)
    blocks = v.reshape(v.shape[:-1] + (-1, 32))
    amax = np.abs(blocks).max(-1, keepdims=True)
    byte = np.maximum(np.where(amax > 0, np.frexp(amax)[1] - 1 + 127, 0) - down, 1)
    scale = np.exp2(byte - 127.0)
    codes = (blocks / scale).astype(np.float32).astype(dtype).astype(np.float64)
    return np.moveaxis((codes * scale).reshape(v.shape), -1, axis)


WIDE = False


def mx_kscale(k, group=512):
    if not WIDE:
        return np.ones(k)
    levels = np.array([18, -18])
    if group != 512:
        return np.exp2(np.random.permutation(np.resize(levels, k // group))).repeat(group)
    if k % 512:
        return np.exp2(np.random.permutation(np.resize(levels, k // 32))).repeat(32)
    a = np.empty((k // 512, 16))
    for p in range(k // 512):
        a[p, :8] = np.random.permutation(np.resize(levels, 8))
        for g in range(8):
            far = levels[np.abs(levels - a[p, g]) >= 10]
            a[p, g + 8] = far[np.random.randint(len(far))]
    return np.exp2(a.ravel()).repeat(32)


def f64(x):
    return np.asarray(x).astype(np.float64)


G, D, M, N = 4, 128, 256, 512


def setup_inputs():
    n = np.random.standard_normal
    s_d = mx_kscale(D, 0)
    return {
        "x": (n((G, D, M)) / s_d[:, None] / np.sqrt(D)).astype(np.float32),
        "c": (n((G, D, N)) * s_d[:, None]).astype(np.float32),
        "gn": (np.random.uniform(0.5, 2.0, (G, 1, N))).astype(np.float32),
    }


def reference(x, c, gn):
    xq = mxq(f64(x), 1, "e4m3")
    cq = mxq(f64(c), 1, "e4m3")
    z = xq.transpose(0, 2, 1) @ cq
    ms = np.mean(np.square(z), axis=-1, keepdims=True)
    y = z / np.sqrt(ms + 1e-05) * f64(gn)
    return y

@@ -1,0 +1,121 @@
+from contextlib import ExitStack
+
+import concourse.mybir as mybir
+
+G, D, M, N = 4, 128, 256, 512
+FLOPS = 2 * G * D * M * N
+
+F32 = mybir.dt.float32
+BF16 = mybir.dt.bfloat16
+U32 = mybir.dt.uint32
+U8 = mybir.dt.uint8
+FP8X4 = mybir.dt.float8_e4m3fn_x4
+ACT = mybir.ActivationFunctionType
+ALU = mybir.AluOpType
+
+P = 128
+PACK = 4
+ROWS = D // PACK
+M_TILE = 128
+HALVES = M // M_TILE
+EPS = 1e-05
+C_VECTOR = 288
+
+
+def interleave(copy, grouped, raw, cols):
+    copy(
+        out=grouped[:, cols, :].rearrange("p (c i) j -> p c j i", i=4),
+        in_=raw[:, :, cols].rearrange("p j (c i) -> p c j i", i=4),
+    )
+
+
+def quantize(nc, codes, scales, grouped, cols):
+    nc.vector.quantize_mx(
+        out=codes[:, cols].bitcast(FP8X4),
+        scales=scales[:, cols],
+        in_=grouped[:, cols, :].rearrange("p w j -> p (w j)"),
+    )
+
+
+def tile_rows_rms_kernel(tc, x, c, gn, out):
+    nc = tc.nc
+    with ExitStack() as ctx:
+        keep = ctx.enter_context(tc.tile_pool(name="keep", bufs=1))
+        psum = ctx.enter_context(tc.psum_pool(name="psum", bufs=1))
+        ctx.enter_context(tc.manual_schedule())
+
+        c_raw = keep.tile([P, PACK, N], F32, align_bytes=64)
+        x_raw = keep.tile([P, PACK, M], F32, align_bytes=64)
+        nc.sync.dma_start(out=c_raw[:], in_=c.rearrange("g (p j) n -> (g p) j n", j=PACK))
+        nc.sync.dma_start(out=x_raw[:], in_=x.rearrange("g (p j) m -> (g p) j m", j=PACK))
+        gains = []
+        for g in range(G):
+            gain = keep.tile([P, N], F32, name="gain%d" % g, align_bytes=64)
+            nc.sync.dma_start(out=gain[:], in_=gn[g, 0, :].partition_broadcast(P))
+            gains.append(gain)
+
+        ones = keep.tile([P, 1], F32, align_bytes=64)
+        eps = keep.tile([P, 1], F32, align_bytes=64)
+        nc.gpsimd.memset(ones[:], 1.0)
+        nc.scalar.activation(out=eps[:], in_=ones[:], func=ACT.Abs_reciprocal_sqrt, scale=1.0 / (EPS * EPS))
+
+        c_grouped = keep.tile([P, N, PACK], BF16, align_bytes=64)
+        x_grouped = keep.tile([P, M, PACK], BF16, align_bytes=64)
+        c_codes = keep.tile([P, N], U32, align_bytes=64)
+        c_scales = keep.tile([P, N], U8, align_bytes=64)
+        x_codes = keep.tile([P, M], U32, align_bytes=64)
+        x_scales = keep.tile([P, M], U8, align_bytes=64)
+
+        interleave(nc.vector.tensor_copy, c_grouped, c_raw, slice(0, C_VECTOR))
+        interleave(nc.scalar.copy, c_grouped, c_raw, slice(C_VECTOR, N))
+        interleave(nc.scalar.copy, x_grouped, x_raw, slice(0, 64))
+        interleave(nc.scalar.copy, x_grouped, x_raw, slice(128, 256))
+        quantize(nc, c_codes, c_scales, c_grouped, slice(0, 256))
+        interleave(nc.vector.tensor_copy, x_grouped, x_raw, slice(64, 128))
+        quantize(nc, c_codes, c_scales, c_grouped, slice(256, 512))
+        quantize(nc, x_codes, x_scales, x_grouped, slice(0, 128))
+        quantize(nc, x_codes, x_scales, x_grouped, slice(128, 256))
+
+        z = {}
+        order = [(g0 + dg, h) for g0 in (0, 2) for h in range(HALVES) for dg in (0, 1)]
+        for g, h in order:
+            if True:
+                rows = slice(g * ROWS, (g + 1) * ROWS)
+                cols = slice(h * M_TILE, (h + 1) * M_TILE)
+                acc = psum.tile([M_TILE, N], F32, name="z%d%d" % (g, h))
+                nc.tensor.matmul_mx(
+                    out=acc[:],
+                    lhsT=x_codes[rows, cols].bitcast(FP8X4),
+                    lhsT_scale=x_scales[rows, cols],
+                    rhs=c_codes[rows, :].bitcast(FP8X4),
+                    rhs_scale=c_scales[rows, :],
+                    start=True,
+                    stop=True,
+                )
+                z[(g, h)] = acc
+
+        sums = keep.tile([P, len(order)], F32, align_bytes=64)
+        inv_rms = keep.tile([P, len(order)], F32, align_bytes=64)
+
+        def square(k):
+            squares = keep.tile([P, N], BF16, name="squares%d" % k, align_bytes=64)
+            nc.scalar.activation(out=squares[:], in_=z[order[k]][:], func=ACT.Square, accum_out=sums[:, k : k + 1])
+
+        def finish(k):
+            g, h = order[k]
+            nc.scalar.activation(
+                out=inv_rms[:, k : k + 1], in_=sums[:, k : k + 1], func=ACT.Abs_reciprocal_sqrt, scale=1.0 / N, bias=eps[:]
+            )
+            y = keep.tile([P, N], F32, name="y%d" % k, align_bytes=64)
+            nc.vector.scalar_tensor_tensor(
+                out=y[:], in0=z[(g, h)][:], scalar=inv_rms[:, k : k + 1], in1=gains[g][:], op0=ALU.mult, op1=ALU.mult
+            )
+            nc.sync.dma_start(out=out[g, h * M_TILE : (h + 1) * M_TILE, :], in_=y[:])
+
+        square(0)
+        finish(0)
+        square(1)
+        for k in range(2, len(order)):
+            square(k)
+            finish(k - 1)
+        finish(len(order) - 1)

@@ -48,11 +48,8 @@ def tile_rows_rms_kernel(tc, x, c, gn, out):
         x_raw = keep.tile([P, PACK, M], F32, align_bytes=64)
         nc.sync.dma_start(out=c_raw[:], in_=c.rearrange("g (p j) n -> (g p) j n", j=PACK))
         nc.sync.dma_start(out=x_raw[:], in_=x.rearrange("g (p j) m -> (g p) j m", j=PACK))
-        gains = []
-        for g in range(G):
-            gain = keep.tile([P, N], F32, name="gain%d" % g, align_bytes=64)
-            nc.sync.dma_start(out=gain[:], in_=gn[g, 0, :].partition_broadcast(P))
-            gains.append(gain)
+        gains = keep.tile([P, G * N], F32, align_bytes=64)
+        nc.sync.dma_start(out=gains[:], in_=gn.rearrange("g o n -> (g o n)").partition_broadcast(P))
 
         ones = keep.tile([P, 1], F32, align_bytes=64)
         eps = keep.tile([P, 1], F32, align_bytes=64)
@@ -77,7 +74,7 @@ def tile_rows_rms_kernel(tc, x, c, gn, out):
         quantize(nc, x_codes, x_scales, x_grouped, slice(128, 256))
 
         z = {}
-        order = [(g0 + dg, h) for g0 in (0, 2) for h in range(HALVES) for dg in (0, 1)]
+        order = [(g, h) for h in range(HALVES) for g in range(G)]
         for g, h in order:
             if True:
                 rows = slice(g * ROWS, (g + 1) * ROWS)
@@ -96,26 +93,40 @@ def tile_rows_rms_kernel(tc, x, c, gn, out):
 
         sums = keep.tile([P, len(order)], F32, align_bytes=64)
         inv_rms = keep.tile([P, len(order)], F32, align_bytes=64)
+        stats = keep.tile([P, 6], F32, align_bytes=64)
+        mean_var = keep.tile([P, 2], F32, align_bytes=64)
+        mean_square = keep.tile([P, 1], F32, align_bytes=64)
 
         def square(k):
             squares = keep.tile([P, N], BF16, name="squares%d" % k, align_bytes=64)
             nc.scalar.activation(out=squares[:], in_=z[order[k]][:], func=ACT.Square, accum_out=sums[:, k : k + 1])
 
+        def root(k, src, scale):
+            nc.scalar.activation(out=inv_rms[:, k : k + 1], in_=src, func=ACT.Abs_reciprocal_sqrt, scale=scale, bias=eps[:])
+
         def finish(k):
             g, h = order[k]
-            nc.scalar.activation(
-                out=inv_rms[:, k : k + 1], in_=sums[:, k : k + 1], func=ACT.Abs_reciprocal_sqrt, scale=1.0 / N, bias=eps[:]
-            )
             y = keep.tile([P, N], F32, name="y%d" % k, align_bytes=64)
             nc.vector.scalar_tensor_tensor(
-                out=y[:], in0=z[(g, h)][:], scalar=inv_rms[:, k : k + 1], in1=gains[g][:], op0=ALU.mult, op1=ALU.mult
+                out=y[:], in0=z[(g, h)][:], scalar=inv_rms[:, k : k + 1], in1=gains[:, g * N : (g + 1) * N], op0=ALU.mult, op1=ALU.mult
             )
             nc.sync.dma_start(out=out[g, h * M_TILE : (h + 1) * M_TILE, :], in_=y[:])
 
         square(0)
+        nc.vector.bn_stats(out=stats[:], in_=z[order[1]][:])
+        nc.vector.bn_aggr(out=mean_var[:], in_=stats[:])
+        nc.vector.scalar_tensor_tensor(
+            out=mean_square[:], in0=mean_var[:, 0:1], scalar=mean_var[:, 0:1], in1=mean_var[:, 1:2], op0=ALU.mult, op1=ALU.add
+        )
+        root(0, sums[:, 0:1], 1.0 / N)
         finish(0)
-        square(1)
-        for k in range(2, len(order)):
+        square(2)
+        root(1, mean_square[:], 1.0)
+        finish(1)
+        for k in range(3, len(order)):
             square(k)
+            root(k - 1, sums[:, k - 1 : k], 1.0 / N)
             finish(k - 1)
-        finish(len(order) - 1)
+        last = len(order) - 1
+        root(last, sums[:, last : last + 1], 1.0 / N)
+        finish(last)

@@ -48,8 +48,11 @@ def tile_rows_rms_kernel(tc, x, c, gn, out):
         x_raw = keep.tile([P, PACK, M], F32, align_bytes=64)
         nc.sync.dma_start(out=c_raw[:], in_=c.rearrange("g (p j) n -> (g p) j n", j=PACK))
         nc.sync.dma_start(out=x_raw[:], in_=x.rearrange("g (p j) m -> (g p) j m", j=PACK))
-        gains = keep.tile([P, G * N], F32, align_bytes=64)
-        nc.sync.dma_start(out=gains[:], in_=gn.rearrange("g o n -> (g o n)").partition_broadcast(P))
+        gains = []
+        for pair in range(G // 2):
+            gain = keep.tile([P, 2 * N], F32, name="gain%d" % pair, align_bytes=64)
+            nc.sync.dma_start(out=gain[:], in_=gn[2 * pair : 2 * pair + 2].rearrange("g o n -> (g o n)").partition_broadcast(P))
+            gains.append(gain)
 
         ones = keep.tile([P, 1], F32, align_bytes=64)
         eps = keep.tile([P, 1], F32, align_bytes=64)
@@ -63,18 +66,19 @@ def tile_rows_rms_kernel(tc, x, c, gn, out):
         x_codes = keep.tile([P, M], U32, align_bytes=64)
         x_scales = keep.tile([P, M], U8, align_bytes=64)
 
-        interleave(nc.vector.tensor_copy, c_grouped, c_raw, slice(0, C_VECTOR))
+        interleave(nc.vector.tensor_copy, c_grouped, c_raw, slice(0, 256))
+        interleave(nc.vector.tensor_copy, c_grouped, c_raw, slice(256, C_VECTOR))
         interleave(nc.scalar.copy, c_grouped, c_raw, slice(C_VECTOR, N))
-        interleave(nc.scalar.copy, x_grouped, x_raw, slice(0, 64))
+        interleave(nc.scalar.copy, x_grouped, x_raw, slice(0, 48))
         interleave(nc.scalar.copy, x_grouped, x_raw, slice(128, 256))
         quantize(nc, c_codes, c_scales, c_grouped, slice(0, 256))
-        interleave(nc.vector.tensor_copy, x_grouped, x_raw, slice(64, 128))
+        interleave(nc.vector.tensor_copy, x_grouped, x_raw, slice(48, 128))
         quantize(nc, c_codes, c_scales, c_grouped, slice(256, 512))
         quantize(nc, x_codes, x_scales, x_grouped, slice(0, 128))
         quantize(nc, x_codes, x_scales, x_grouped, slice(128, 256))
 
         z = {}
-        order = [(g, h) for h in range(HALVES) for g in range(G)]
+        order = [(g0 + dg, h) for g0 in (0, 2) for h in range(HALVES) for dg in (0, 1)]
         for g, h in order:
             if True:
                 rows = slice(g * ROWS, (g + 1) * ROWS)
@@ -104,13 +108,16 @@ def tile_rows_rms_kernel(tc, x, c, gn, out):
         def root(k, src, scale):
             nc.scalar.activation(out=inv_rms[:, k : k + 1], in_=src, func=ACT.Abs_reciprocal_sqrt, scale=scale, bias=eps[:])
 
-        def finish(k):
+        def finish(k, pieces=1):
             g, h = order[k]
-            y = keep.tile([P, N], F32, name="y%d" % k, align_bytes=64)
-            nc.vector.scalar_tensor_tensor(
-                out=y[:], in0=z[(g, h)][:], scalar=inv_rms[:, k : k + 1], in1=gains[:, g * N : (g + 1) * N], op0=ALU.mult, op1=ALU.mult
-            )
-            nc.sync.dma_start(out=out[g, h * M_TILE : (h + 1) * M_TILE, :], in_=y[:])
+            width = N // pieces
+            for n0 in range(0, N, width):
+                y = keep.tile([P, width], F32, name="y%d_%d" % (k, n0), align_bytes=64)
+                g0 = (g % 2) * N + n0
+                nc.vector.scalar_tensor_tensor(
+                    out=y[:], in0=z[(g, h)][:, n0 : n0 + width], scalar=inv_rms[:, k : k + 1], in1=gains[g // 2][:, g0 : g0 + width], op0=ALU.mult, op1=ALU.mult
+                )
+                nc.sync.dma_start(out=out[g, h * M_TILE : (h + 1) * M_TILE, n0 : n0 + width], in_=y[:])
 
         square(0)
         nc.vector.bn_stats(out=stats[:], in_=z[order[1]][:])
@@ -129,4 +136,4 @@ def tile_rows_rms_kernel(tc, x, c, gn, out):
             finish(k - 1)
         last = len(order) - 1
         root(last, sums[:, last : last + 1], 1.0 / N)
-        finish(last)
+        finish(last, 2)

@@ -4,6 +4,7 @@ import concourse.mybir as mybir
 
 G, D, M, N = 4, 128, 256, 512
 FLOPS = 2 * G * D * M * N
+EPS = 1e-05
 
 F32 = mybir.dt.float32
 BF16 = mybir.dt.bfloat16
@@ -17,15 +18,21 @@ P = 128
 PACK = 4
 ROWS = D // PACK
 M_TILE = 128
-HALVES = M // M_TILE
-EPS = 1e-05
-C_VECTOR = 288
+M_TILES = M // M_TILE
+C_HALF = N // 2
+RUN = 4
+ALIGN = 64
+BN_STATS = 6
+
+C_VECTOR = 176
+X_SCALAR = 64
+LAST_PIECES = 2
 
 
-def interleave(copy, grouped, raw, cols):
+def interleave(copy, grouped, raw, first, cols):
     copy(
-        out=grouped[:, cols, :].rearrange("p (c i) j -> p c j i", i=4),
-        in_=raw[:, :, cols].rearrange("p j (c i) -> p c j i", i=4),
+        out=grouped[:, first + cols.start : first + cols.stop, :].rearrange("p (c i) j -> p c j i", i=RUN),
+        in_=raw[:, :, cols].rearrange("p j (c i) -> p c j i", i=RUN),
     )
 
 
@@ -44,86 +51,107 @@ def tile_rows_rms_kernel(tc, x, c, gn, out):
         psum = ctx.enter_context(tc.psum_pool(name="psum", bufs=1))
         ctx.enter_context(tc.manual_schedule())
 
-        c_raw = keep.tile([P, PACK, N], F32, align_bytes=64)
-        x_raw = keep.tile([P, PACK, M], F32, align_bytes=64)
-        nc.sync.dma_start(out=c_raw[:], in_=c.rearrange("g (p j) n -> (g p) j n", j=PACK))
-        nc.sync.dma_start(out=x_raw[:], in_=x.rearrange("g (p j) m -> (g p) j m", j=PACK))
+        c_rows = c.rearrange("g (p j) n -> (g p) j n", j=PACK)
+        x_rows = x.rearrange("g (p j) m -> (g p) j m", j=PACK)
+        c_raw = []
+        x_raw = []
+        for half in range(2):
+            raw = keep.tile([P, PACK, C_HALF], F32, name="c_raw%d" % half, align_bytes=ALIGN)
+            nc.sync.dma_start(out=raw[:], in_=c_rows[:, :, half * C_HALF : (half + 1) * C_HALF])
+            c_raw.append(raw)
+        for h in range(M_TILES):
+            raw = keep.tile([P, PACK, M_TILE], F32, name="x_raw%d" % h, align_bytes=ALIGN)
+            nc.sync.dma_start(out=raw[:], in_=x_rows[:, :, h * M_TILE : (h + 1) * M_TILE])
+            x_raw.append(raw)
         gains = []
         for pair in range(G // 2):
-            gain = keep.tile([P, 2 * N], F32, name="gain%d" % pair, align_bytes=64)
-            nc.sync.dma_start(out=gain[:], in_=gn[2 * pair : 2 * pair + 2].rearrange("g o n -> (g o n)").partition_broadcast(P))
+            gain = keep.tile([P, 2 * N], F32, name="gain%d" % pair, align_bytes=ALIGN)
+            row = gn[2 * pair : 2 * pair + 2].rearrange("g o n -> (g o n)")
+            nc.sync.dma_start(out=gain[:], in_=row.partition_broadcast(P))
             gains.append(gain)
 
-        ones = keep.tile([P, 1], F32, align_bytes=64)
-        eps = keep.tile([P, 1], F32, align_bytes=64)
+        ones = keep.tile([P, 1], F32, align_bytes=ALIGN)
+        eps = keep.tile([P, 1], F32, align_bytes=ALIGN)
         nc.gpsimd.memset(ones[:], 1.0)
         nc.scalar.activation(out=eps[:], in_=ones[:], func=ACT.Abs_reciprocal_sqrt, scale=1.0 / (EPS * EPS))
 
-        c_grouped = keep.tile([P, N, PACK], BF16, align_bytes=64)
-        x_grouped = keep.tile([P, M, PACK], BF16, align_bytes=64)
-        c_codes = keep.tile([P, N], U32, align_bytes=64)
-        c_scales = keep.tile([P, N], U8, align_bytes=64)
-        x_codes = keep.tile([P, M], U32, align_bytes=64)
-        x_scales = keep.tile([P, M], U8, align_bytes=64)
+        c_grouped = keep.tile([P, N, PACK], BF16, align_bytes=ALIGN)
+        x_grouped = keep.tile([P, M, PACK], BF16, align_bytes=ALIGN)
+        c_codes = keep.tile([P, N], U32, align_bytes=ALIGN)
+        c_scales = keep.tile([P, N], U8, align_bytes=ALIGN)
+        x_codes = keep.tile([P, M], U32, align_bytes=ALIGN)
+        x_scales = keep.tile([P, M], U8, align_bytes=ALIGN)
 
-        interleave(nc.vector.tensor_copy, c_grouped, c_raw, slice(0, 256))
-        interleave(nc.vector.tensor_copy, c_grouped, c_raw, slice(256, C_VECTOR))
-        interleave(nc.scalar.copy, c_grouped, c_raw, slice(C_VECTOR, N))
-        interleave(nc.scalar.copy, x_grouped, x_raw, slice(0, 48))
-        interleave(nc.scalar.copy, x_grouped, x_raw, slice(128, 256))
-        quantize(nc, c_codes, c_scales, c_grouped, slice(0, 256))
-        interleave(nc.vector.tensor_copy, x_grouped, x_raw, slice(48, 128))
-        quantize(nc, c_codes, c_scales, c_grouped, slice(256, 512))
-        quantize(nc, x_codes, x_scales, x_grouped, slice(0, 128))
-        quantize(nc, x_codes, x_scales, x_grouped, slice(128, 256))
+        interleave(nc.vector.tensor_copy, c_grouped, c_raw[0], 0, slice(0, C_VECTOR))
+        interleave(nc.scalar.copy, c_grouped, c_raw[0], 0, slice(C_VECTOR, C_HALF))
+        quantize(nc, c_codes, c_scales, c_grouped, slice(0, C_HALF))
+        interleave(nc.vector.tensor_copy, c_grouped, c_raw[1], C_HALF, slice(0, C_VECTOR))
+        interleave(nc.scalar.copy, c_grouped, c_raw[1], C_HALF, slice(C_VECTOR, C_HALF))
+        interleave(nc.scalar.copy, x_grouped, x_raw[0], 0, slice(0, X_SCALAR))
+        interleave(nc.vector.tensor_copy, x_grouped, x_raw[0], 0, slice(X_SCALAR, M_TILE))
+        interleave(nc.scalar.copy, x_grouped, x_raw[1], M_TILE, slice(0, M_TILE))
+        quantize(nc, c_codes, c_scales, c_grouped, slice(C_HALF, N))
+        quantize(nc, x_codes, x_scales, x_grouped, slice(0, M_TILE))
+        quantize(nc, x_codes, x_scales, x_grouped, slice(M_TILE, M))
 
-        z = {}
-        order = [(g0 + dg, h) for g0 in (0, 2) for h in range(HALVES) for dg in (0, 1)]
+        order = [(2 * pair + dg, h) for pair in range(G // 2) for h in range(M_TILES) for dg in range(2)]
+        z = []
         for g, h in order:
-            if True:
-                rows = slice(g * ROWS, (g + 1) * ROWS)
-                cols = slice(h * M_TILE, (h + 1) * M_TILE)
-                acc = psum.tile([M_TILE, N], F32, name="z%d%d" % (g, h))
-                nc.tensor.matmul_mx(
-                    out=acc[:],
-                    lhsT=x_codes[rows, cols].bitcast(FP8X4),
-                    lhsT_scale=x_scales[rows, cols],
-                    rhs=c_codes[rows, :].bitcast(FP8X4),
-                    rhs_scale=c_scales[rows, :],
-                    start=True,
-                    stop=True,
-                )
-                z[(g, h)] = acc
+            rows = slice(g * ROWS, (g + 1) * ROWS)
+            cols = slice(h * M_TILE, (h + 1) * M_TILE)
+            acc = psum.tile([M_TILE, N], F32, name="z%d%d" % (g, h))
+            nc.tensor.matmul_mx(
+                out=acc[:],
+                lhsT=x_codes[rows, cols].bitcast(FP8X4),
+                lhsT_scale=x_scales[rows, cols],
+                rhs=c_codes[rows, :].bitcast(FP8X4),
+                rhs_scale=c_scales[rows, :],
+                start=True,
+                stop=True,
+            )
+            z.append(acc)
 
-        sums = keep.tile([P, len(order)], F32, align_bytes=64)
-        inv_rms = keep.tile([P, len(order)], F32, align_bytes=64)
-        stats = keep.tile([P, 6], F32, align_bytes=64)
-        mean_var = keep.tile([P, 2], F32, align_bytes=64)
-        mean_square = keep.tile([P, 1], F32, align_bytes=64)
+        sums = keep.tile([P, len(order)], F32, align_bytes=ALIGN)
+        inv_rms = keep.tile([P, len(order)], F32, align_bytes=ALIGN)
+        stats = keep.tile([P, BN_STATS], F32, align_bytes=ALIGN)
+        mean_var = keep.tile([P, 2], F32, align_bytes=ALIGN)
+        mean_square = keep.tile([P, 1], F32, align_bytes=ALIGN)
 
         def square(k):
-            squares = keep.tile([P, N], BF16, name="squares%d" % k, align_bytes=64)
-            nc.scalar.activation(out=squares[:], in_=z[order[k]][:], func=ACT.Square, accum_out=sums[:, k : k + 1])
+            squares = keep.tile([P, N], BF16, name="squares%d" % k, align_bytes=ALIGN)
+            nc.scalar.activation(out=squares[:], in_=z[k][:], func=ACT.Square, accum_out=sums[:, k : k + 1])
 
         def root(k, src, scale):
-            nc.scalar.activation(out=inv_rms[:, k : k + 1], in_=src, func=ACT.Abs_reciprocal_sqrt, scale=scale, bias=eps[:])
+            nc.scalar.activation(
+                out=inv_rms[:, k : k + 1], in_=src, func=ACT.Abs_reciprocal_sqrt, scale=scale, bias=eps[:]
+            )
 
         def finish(k, pieces=1):
             g, h = order[k]
             width = N // pieces
             for n0 in range(0, N, width):
-                y = keep.tile([P, width], F32, name="y%d_%d" % (k, n0), align_bytes=64)
-                g0 = (g % 2) * N + n0
+                y = keep.tile([P, width], F32, name="y%d_%d" % (k, n0), align_bytes=ALIGN)
+                gain_col = (g % 2) * N + n0
                 nc.vector.scalar_tensor_tensor(
-                    out=y[:], in0=z[(g, h)][:, n0 : n0 + width], scalar=inv_rms[:, k : k + 1], in1=gains[g // 2][:, g0 : g0 + width], op0=ALU.mult, op1=ALU.mult
+                    out=y[:],
+                    in0=z[k][:, n0 : n0 + width],
+                    scalar=inv_rms[:, k : k + 1],
+                    in1=gains[g // 2][:, gain_col : gain_col + width],
+                    op0=ALU.mult,
+                    op1=ALU.mult,
                 )
                 nc.sync.dma_start(out=out[g, h * M_TILE : (h + 1) * M_TILE, n0 : n0 + width], in_=y[:])
 
         square(0)
-        nc.vector.bn_stats(out=stats[:], in_=z[order[1]][:])
+        nc.vector.bn_stats(out=stats[:], in_=z[1][:])
         nc.vector.bn_aggr(out=mean_var[:], in_=stats[:])
         nc.vector.scalar_tensor_tensor(
-            out=mean_square[:], in0=mean_var[:, 0:1], scalar=mean_var[:, 0:1], in1=mean_var[:, 1:2], op0=ALU.mult, op1=ALU.add
+            out=mean_square[:],
+            in0=mean_var[:, 0:1],
+            scalar=mean_var[:, 0:1],
+            in1=mean_var[:, 1:2],
+            op0=ALU.mult,
+            op1=ALU.add,
         )
         root(0, sums[:, 0:1], 1.0 / N)
         finish(0)
@@ -136,4 +164,4 @@ def tile_rows_rms_kernel(tc, x, c, gn, out):
             finish(k - 1)
         last = len(order) - 1
         root(last, sums[:, last : last + 1], 1.0 / N)
-        finish(last, 2)
+        finish(last, LAST_PIECES)

from contextlib import ExitStack

import concourse.mybir as mybir

G, D, M, N = 4, 128, 256, 512
FLOPS = 2 * G * D * M * N
EPS = 1e-05

F32 = mybir.dt.float32
BF16 = mybir.dt.bfloat16
U32 = mybir.dt.uint32
U8 = mybir.dt.uint8
FP8X4 = mybir.dt.float8_e4m3fn_x4
ACT = mybir.ActivationFunctionType
ALU = mybir.AluOpType

P = 128
PACK = 4
ROWS = D // PACK
M_TILE = 128
M_TILES = M // M_TILE
C_HALF = N // 2
RUN = 4
ALIGN = 64
BN_STATS = 6

C_VECTOR = 176
X_SCALAR = 64
LAST_PIECES = 2


def interleave(copy, grouped, raw, first, cols):
    copy(
        out=grouped[:, first + cols.start : first + cols.stop, :].rearrange("p (c i) j -> p c j i", i=RUN),
        in_=raw[:, :, cols].rearrange("p j (c i) -> p c j i", i=RUN),
    )


def quantize(nc, codes, scales, grouped, cols):
    nc.vector.quantize_mx(
        out=codes[:, cols].bitcast(FP8X4),
        scales=scales[:, cols],
        in_=grouped[:, cols, :].rearrange("p w j -> p (w j)"),
    )


def tile_rows_rms_kernel(tc, x, c, gn, out):
    nc = tc.nc
    with ExitStack() as ctx:
        keep = ctx.enter_context(tc.tile_pool(name="keep", bufs=1))
        psum = ctx.enter_context(tc.psum_pool(name="psum", bufs=1))
        ctx.enter_context(tc.manual_schedule())

        c_rows = c.rearrange("g (p j) n -> (g p) j n", j=PACK)
        x_rows = x.rearrange("g (p j) m -> (g p) j m", j=PACK)
        c_raw = []
        x_raw = []
        for half in range(2):
            raw = keep.tile([P, PACK, C_HALF], F32, name="c_raw%d" % half, align_bytes=ALIGN)
            nc.sync.dma_start(out=raw[:], in_=c_rows[:, :, half * C_HALF : (half + 1) * C_HALF])
            c_raw.append(raw)
        for h in range(M_TILES):
            raw = keep.tile([P, PACK, M_TILE], F32, name="x_raw%d" % h, align_bytes=ALIGN)
            nc.sync.dma_start(out=raw[:], in_=x_rows[:, :, h * M_TILE : (h + 1) * M_TILE])
            x_raw.append(raw)
        gains = []
        for pair in range(G // 2):
            gain = keep.tile([P, 2 * N], F32, name="gain%d" % pair, align_bytes=ALIGN)
            row = gn[2 * pair : 2 * pair + 2].rearrange("g o n -> (g o n)")
            nc.sync.dma_start(out=gain[:], in_=row.partition_broadcast(P))
            gains.append(gain)

        ones = keep.tile([P, 1], F32, align_bytes=ALIGN)
        eps = keep.tile([P, 1], F32, align_bytes=ALIGN)
        nc.gpsimd.memset(ones[:], 1.0)
        nc.scalar.activation(out=eps[:], in_=ones[:], func=ACT.Abs_reciprocal_sqrt, scale=1.0 / (EPS * EPS))

        c_grouped = keep.tile([P, N, PACK], BF16, align_bytes=ALIGN)
        x_grouped = keep.tile([P, M, PACK], BF16, align_bytes=ALIGN)
        c_codes = keep.tile([P, N], U32, align_bytes=ALIGN)
        c_scales = keep.tile([P, N], U8, align_bytes=ALIGN)
        x_codes = keep.tile([P, M], U32, align_bytes=ALIGN)
        x_scales = keep.tile([P, M], U8, align_bytes=ALIGN)

        interleave(nc.vector.tensor_copy, c_grouped, c_raw[0], 0, slice(0, C_VECTOR))
        interleave(nc.scalar.copy, c_grouped, c_raw[0], 0, slice(C_VECTOR, C_HALF))
        quantize(nc, c_codes, c_scales, c_grouped, slice(0, C_HALF))
        interleave(nc.vector.tensor_copy, c_grouped, c_raw[1], C_HALF, slice(0, C_VECTOR))
        interleave(nc.scalar.copy, c_grouped, c_raw[1], C_HALF, slice(C_VECTOR, C_HALF))
        interleave(nc.scalar.copy, x_grouped, x_raw[0], 0, slice(0, X_SCALAR))
        interleave(nc.vector.tensor_copy, x_grouped, x_raw[0], 0, slice(X_SCALAR, M_TILE))
        interleave(nc.scalar.copy, x_grouped, x_raw[1], M_TILE, slice(0, M_TILE))
        quantize(nc, c_codes, c_scales, c_grouped, slice(C_HALF, N))
        quantize(nc, x_codes, x_scales, x_grouped, slice(0, M_TILE))
        quantize(nc, x_codes, x_scales, x_grouped, slice(M_TILE, M))

        order = [(2 * pair + dg, h) for pair in range(G // 2) for h in range(M_TILES) for dg in range(2)]
        z = []
        for g, h in order:
            rows = slice(g * ROWS, (g + 1) * ROWS)
            cols = slice(h * M_TILE, (h + 1) * M_TILE)
            acc = psum.tile([M_TILE, N], F32, name="z%d%d" % (g, h))
            nc.tensor.matmul_mx(
                out=acc[:],
                lhsT=x_codes[rows, cols].bitcast(FP8X4),
                lhsT_scale=x_scales[rows, cols],
                rhs=c_codes[rows, :].bitcast(FP8X4),
                rhs_scale=c_scales[rows, :],
                start=True,
                stop=True,
            )
            z.append(acc)

        sums = keep.tile([P, len(order)], F32, align_bytes=ALIGN)
        inv_rms = keep.tile([P, len(order)], F32, align_bytes=ALIGN)
        stats = keep.tile([P, BN_STATS], F32, align_bytes=ALIGN)
        mean_var = keep.tile([P, 2], F32, align_bytes=ALIGN)
        mean_square = keep.tile([P, 1], F32, align_bytes=ALIGN)

        def square(k):
            squares = keep.tile([P, N], BF16, name="squares%d" % k, align_bytes=ALIGN)
            nc.scalar.activation(out=squares[:], in_=z[k][:], func=ACT.Square, accum_out=sums[:, k : k + 1])

        def root(k, src, scale):
            nc.scalar.activation(
                out=inv_rms[:, k : k + 1], in_=src, func=ACT.Abs_reciprocal_sqrt, scale=scale, bias=eps[:]
            )

        def finish(k, pieces=1):
            g, h = order[k]
            width = N // pieces
            for n0 in range(0, N, width):
                y = keep.tile([P, width], F32, name="y%d_%d" % (k, n0), align_bytes=ALIGN)
                gain_col = (g % 2) * N + n0
                nc.vector.scalar_tensor_tensor(
                    out=y[:],
                    in0=z[k][:, n0 : n0 + width],
                    scalar=inv_rms[:, k : k + 1],
                    in1=gains[g // 2][:, gain_col : gain_col + width],
                    op0=ALU.mult,
                    op1=ALU.mult,
                )
                nc.sync.dma_start(out=out[g, h * M_TILE : (h + 1) * M_TILE, n0 : n0 + width], in_=y[:])

        square(0)
        nc.vector.bn_stats(out=stats[:], in_=z[1][:])
        nc.vector.bn_aggr(out=mean_var[:], in_=stats[:])
        nc.vector.scalar_tensor_tensor(
            out=mean_square[:],
            in0=mean_var[:, 0:1],
            scalar=mean_var[:, 0:1],
            in1=mean_var[:, 1:2],
            op0=ALU.mult,
            op1=ALU.add,
        )
        root(0, sums[:, 0:1], 1.0 / N)
        finish(0)
        square(2)
        root(1, mean_square[:], 1.0)
        finish(1)
        for k in range(3, len(order)):
            square(k)
            root(k - 1, sums[:, k - 1 : k], 1.0 / N)
            finish(k - 1)
        last = len(order) - 1
        root(last, sums[:, last : last + 1], 1.0 / N)
        finish(last, LAST_PIECES)
